import numpy as np
import ml_dtypes


def mxq(x, axis, fmt="e4m3"):
    dtype, down = {"e4m3": (ml_dtypes.float8_e4m3fn, 7), "e5m2": (ml_dtypes.float8_e5m2, 14)}[fmt]
    v = np.moveaxis(np.asarray(x, np.float32).astype(ml_dtypes.bfloat16).astype(np.float64), axis, -1)
    blocks = v.reshape(v.shape[:-1] + (-1, 32))
    amax = np.abs(blocks).max(-1, keepdims=True)
    byte = np.maximum(np.where(amax > 0, np.frexp(amax)[1] - 1 + 127, 0) - down, 1)
    scale = np.exp2(byte - 127.0)
    codes = (blocks / scale).astype(np.float32).astype(dtype).astype(np.float64)
    return np.moveaxis((codes * scale).reshape(v.shape), -1, axis)


WIDE = False


def mx_kscale(k):
    if not WIDE:
        return np.ones(k)
    levels = np.array([10, -10, 5, -5, 0])
    if k % 512:
        return np.exp2(np.random.permutation(np.resize(levels, k // 32))).repeat(32)
    a = np.empty((k // 512, 16))
    for p in range(k // 512):
        a[p, :8] = np.random.permutation(np.resize(levels, 8))
        for g in range(8):
            far = levels[np.abs(levels - a[p, g]) >= 10]
            a[p, g + 8] = far[np.random.randint(len(far))]
    return np.exp2(a.ravel()).repeat(32)


def f64(x):
    return np.asarray(x).astype(np.float64)


def striped(idx):
    return np.tile(idx.reshape(-1, 16).T, (8, 1)).astype(np.uint16)


def unstriped(offs):
    return offs[:16].T.reshape(-1).astype(np.int64)


def striped8(idx):
    return np.concatenate([x.reshape(-1, 16).T for x in idx]).astype(np.uint16)


def runs(offs, k):
    lists = np.stack([offs[16 * r : 16 * r + 16].T.reshape(-1) for r in range(8)]).astype(np.int64)
    return lists[np.arange(k) % 512 // 64]


def pack_weight(w):
    k, n = w.shape
    w = f64(np.asarray(w, np.float32).astype(ml_dtypes.bfloat16)).reshape(k // 32, 32, n)
    amax = np.abs(w).max(1)
    byte = np.clip(np.where(amax > 0, np.frexp(amax)[1] - 1 + 127 - 7, 1), 1, 254)
    scaled = (w * np.exp2(127.0 - byte)[:, None, :]).reshape(k, n).astype(np.float32)
    words = np.ascontiguousarray(scaled.reshape(k // 512, 128, 4, n).transpose(0, 1, 3, 2)).astype(ml_dtypes.float8_e4m3fn).view(np.uint8)
    return words, np.ascontiguousarray(byte.astype(np.uint8).reshape(k // 512, 16, n))


def unpack_weight(words, scales):
    g, p, n, _ = words.shape
    vals = np.ascontiguousarray(words).view(ml_dtypes.float8_e4m3fn).astype(np.float64) * np.repeat(np.exp2(scales.astype(np.float64) - 127.0), 8, axis=1)[..., None]
    return vals.transpose(0, 1, 3, 2).reshape(g * 512, n)


def sigmoid(v):
    return 1.0 / (1.0 + np.exp(-np.maximum(v, -700.0)))

def planes(y):
    n, m = y.shape
    v = y.astype(np.float32).astype(ml_dtypes.bfloat16).astype(np.float64).reshape(n // 32, 32, m)
    top = np.abs(v).max(1)
    byte = np.clip(np.where(top > 0, np.frexp(top)[1] - 1 + 127 - 7, 1), 1, 254)
    codes = (v * np.exp2(127.0 - byte)[:, None, :]).reshape(n, m).astype(np.float32).astype(ml_dtypes.float8_e4m3fn).view(np.uint8)
    words = codes.reshape(n // 512, 128, 4, m).transpose(0, 1, 3, 2)
    return np.ascontiguousarray(words), np.ascontiguousarray(byte.astype(np.uint8).reshape(n // 512, 16, m))


K, T, S, N, H, U = 512, 2048, 512, 512, 512, 1024


def setup_inputs():
    n = np.random.standard_normal
    s = mx_kscale(K)[:, None]
    u = mx_kscale(H)
    packed_xT = pack_weight(n((K, T)) * s)
    packed_w1 = pack_weight(n((K, H)) / np.sqrt(K) / s)
    packed_w2 = pack_weight(n((K, H)) / np.sqrt(K) / s)
    packed_w3 = pack_weight(n((H, N)) / np.sqrt(H) / u[:, None])
    return {
        "x_words": packed_xT[0],
        "x_scales": packed_xT[1],
        "w1_words": packed_w1[0],
        "w1_scales": packed_w1[1],
        "w2_words": packed_w2[0],
        "w2_scales": packed_w2[1],
        "gn": (np.random.uniform(0.5, 1.5, (H, 1)) * u[:, None]).astype(np.float32),
        "w3_words": packed_w3[0],
        "w3_scales": packed_w3[1],
        "mem": n((N, U)).astype(np.float32),
        "offs": striped(np.random.permutation(T)[:S]),
        "hz": striped8(np.random.randint(0, T, (8, S))),
        "n1": striped(np.random.permutation(S)),
        "n2": striped(np.random.permutation(S)),
        "n3": striped(np.random.permutation(U)[:S]),
    }


def reference(x_words, x_scales, w1_words, w1_scales, w2_words, w2_scales, gn, w3_words, w3_scales, mem, offs, hz, n1, n2, n3):
    old = f64(mem)[:, unstriped(n3)]
    xq = unpack_weight(x_words, x_scales)[:, unstriped(offs)]
    y = unpack_weight(w1_words, w1_scales).T @ xq
    x_hz = unpack_weight(x_words, x_scales)[np.arange(K)[:, None], runs(hz, K)]
    d = unpack_weight(w2_words, w2_scales).T @ x_hz
    z = f64(gn) * (0.75 * (y * d[:, unstriped(n2)] - (y[:, unstriped(n1)] * d)))
    h = unpack_weight(w3_words, w3_scales).T @ mxq(z, 0, "e4m3")
    nw = old + sigmoid(h) * (h - old)
    out = f64(mem).copy()
    out[:, unstriped(n3)] = nw
    return (out,) + planes(out)

@@ -1,0 +1,238 @@
+from contextlib import ExitStack
+
+import concourse.mybir as mybir
+
+K, T, S, N, H, U = 512, 2048, 512, 512, 512, 1024
+FLOPS = 3 * 2 * 512 * 512 * 512
+
+F32 = mybir.dt.float32
+BF16 = mybir.dt.bfloat16
+I32 = mybir.dt.int32
+U32 = mybir.dt.uint32
+U16 = mybir.dt.uint16
+U8 = mybir.dt.uint8
+FP8X4 = mybir.dt.float8_e4m3fn_x4
+ACT = mybir.ActivationFunctionType
+ALU = mybir.AluOpType
+
+P = 128
+PACK = 4
+HALF = S // 2
+STRIPE = 16
+
+
+def tile_picked_twhcrossbpaget_none_po_kernel(
+    tc, x_words, x_scales, w1_words, w1_scales, w2_words, w2_scales, gn, w3_words, w3_scales, mem, offs, hz, n1, n2, n3,
+    out_0, out_1, out_2,
+):
+    nc = tc.nc
+
+    def words_of(packed):
+        return packed[0].rearrange("p n r -> p (n r)").bitcast(I32)
+
+    with ExitStack() as ctx:
+        keep = ctx.enter_context(tc.tile_pool(name="keep", bufs=1))
+        psum = ctx.enter_context(tc.psum_pool(name="psum", bufs=1))
+
+        def sb(name, shape, dtype, tag=None):
+            return keep.tile(shape, dtype, name=name, tag=tag or name, align_bytes=64)
+
+        offs_t = sb("offs_t", [P, S // STRIPE], U16)
+        hz_t = sb("hz_t", [P, S // STRIPE], U16)
+        n1_t = sb("n1_t", [P, S // STRIPE], U16)
+        n2_t = sb("n2_t", [P, S // STRIPE], U16)
+        n3_t = sb("n3_t", [P, S // STRIPE], U16)
+        xw = sb("xw", [P, T], U32)
+        xs = sb("xs", [P, T], U8)
+        w_raw = [sb(f"w_raw{i}", [P, H], U32) for i in range(2)]
+        w_dealt = [sb(f"w_dealt{i}", [P, H], U32) for i in range(2)]
+        s_raw = [sb(f"s_raw{i}", [P, H], U8) for i in range(2)]
+        s_dealt = []
+        gn_t = sb("gn_t", [P, PACK], F32)
+        gain = sb("gain", [P, PACK], F32)
+        page = [sb(f"page{t}", [P, U], F32) for t in range(PACK)]
+        mem_rows = mem.rearrange("(p t) u -> p t u", t=PACK)
+        out_rows = out_0.rearrange("(p t) u -> p t u", t=PACK)
+
+        nc.vector.memset(xs[:].bitcast(I32), 0)
+        nc.gpsimd.memset(s_raw[0][:].bitcast(I32), 0)
+        nc.vector.memset(s_raw[1][:].bitcast(I32), 0)
+
+        def load_scale_rows(queue, tile, scales):
+            for a in range(4):
+                queue.dma_start(out=tile[a:P:32, :].bitcast(I32), in_=scales[0][a:16:4, :].bitcast(I32))
+
+        xsc = x_scales[0]
+        nc.scalar.dma_start(out=xs[0:P:16, :].bitcast(I32), in_=xsc[0:16:2, :].bitcast(I32))
+        nc.scalar.dma_start(out=xs[1:P:16, :].bitcast(I32), in_=xsc[1:16:2, :].bitcast(I32))
+        nc.scalar.dma_start(out=xs[2:P:32, :].bitcast(I32), in_=xsc[2:16:4, :].bitcast(I32))
+        nc.scalar.dma_start(out=xs[3:P:32, :].bitcast(I32), in_=xsc[3:16:4, :].bitcast(I32))
+        load_scale_rows(nc.gpsimd, s_raw[0], w1_scales)
+        nc.sync.dma_start(hz_t[:], hz)
+        nc.sync.dma_start(offs_t[:], offs)
+        nc.sync.dma_start(out=gn_t[:], in_=gn.rearrange("(p t) o -> p (t o)", t=PACK))
+        nc.sync.dma_start(n3_t[:], n3)
+        nc.sync.dma_start(out=xw[:].bitcast(I32), in_=words_of(x_words))
+        nc.sync.dma_start(out=w_raw[0][:].bitcast(I32), in_=words_of(w1_words))
+        nc.scalar.activation(gain[:], gn_t[:], ACT.Copy, scale=0.75)
+        nc.sync.dma_start(out=page[0][:], in_=mem_rows[:, 0, :])
+        nc.sync.dma_start(n1_t[:], n1)
+        nc.sync.dma_start(n2_t[:], n2)
+        nc.sync.dma_start(out=page[1][:], in_=mem_rows[:, 1, :])
+        nc.sync.dma_start(out=w_raw[1][:].bitcast(I32), in_=words_of(w2_words))
+        load_scale_rows(nc.sync, s_raw[1], w2_scales)
+        nc.sync.dma_start(out=page[2][:], in_=mem_rows[:, 2, :])
+        nc.sync.dma_start(out=page[3][:], in_=mem_rows[:, 3, :])
+
+        hz_bytes = sb("hz_bytes", [P, S], U8)
+        hz_plane = sb("hz_plane", [P, S], U8)
+        offs_plane = sb("offs_plane", [P, S], U8)
+        offs_words = sb("offs_words", [P, S], U32)
+        hz_words = sb("hz_words", [P, S], U32)
+
+        def dealt_view(tile):
+            return tile.rearrange("p (t m) -> p m t", t=PACK)
+
+        def raw_view(tile):
+            return tile.rearrange("p (m t) -> p m t", t=PACK)
+
+        nc.vector.tensor_copy(hz_bytes[:], xs[:].indirect(hz_t[:]))
+        nc.vector.tensor_copy(hz_plane[:].bitcast(I32), hz_bytes[:].bitcast(I32))
+        for e in range(2):
+            nc.sync.dma_start(out=hz_plane[2 + e : P : 32, :].bitcast(I32), in_=hz_bytes[16 + e : P : 32, :].bitcast(I32))
+        nc.vector.tensor_copy(offs_plane[:], xs[:].indirect(offs_t[:]))
+        nc.vector.tensor_copy(offs_words[:], xw[:].indirect(offs_t[:]))
+        s_dealt.append(sb("s1_dealt", [P, H], U8, tag="xs"))
+        nc.vector.tensor_copy(dealt_view(s_dealt[0][:]), raw_view(s_raw[0][:]))
+        nc.vector.tensor_copy(hz_words[:], xw[:].indirect(hz_t[:]))
+        s_dealt.append(sb("s2_dealt", [P, H], U8, tag="hz_bytes"))
+        nc.vector.tensor_copy(dealt_view(s_dealt[1][:]), raw_view(s_raw[1][:]))
+        nc.scalar.copy(dealt_view(w_dealt[0][:]), raw_view(w_raw[0][:]))
+        w_raw.append(sb("w_raw2", [P, H], U32, tag="w_raw0"))
+        s_raw.append(sb("s_raw2", [P, H], U8, tag="s_raw0"))
+        s_dealt.append(sb("s3_dealt", [P, H], U8))
+        nc.sync.dma_start(out=w_raw[2][:].bitcast(I32), in_=words_of(w3_words))
+        nc.gpsimd.memset(s_raw[2][:].bitcast(I32), 0)
+        load_scale_rows(nc.sync, s_raw[2], w3_scales)
+        nc.gpsimd.tensor_copy(w_dealt[1][:].rearrange("p (t m) -> p t m", t=PACK), w_raw[1][:].rearrange("p (m t) -> p t m", t=PACK))
+        nc.gpsimd.tensor_copy(dealt_view(s_dealt[2][:]), raw_view(s_raw[2][:]))
+
+        def product(out, w, w_scale, t, rhs, rhs_scale):
+            cols = slice(t * P, (t + 1) * P)
+            nc.tensor.matmul_mx(
+                out=out, lhsT=w[:, cols].bitcast(FP8X4), lhsT_scale=w_scale[:, cols],
+                rhs=rhs.bitcast(FP8X4), rhs_scale=rhs_scale, start=True, stop=True,
+            )
+
+        ys = sb("ys", [P, PACK, S], F32)
+        ds = sb("ds", [P, PACK, S], F32)
+        old = sb("old", [P, PACK, S], F32)
+        y_bank = [psum.tile([P, S], F32, name=f"y_bank{t}", tag=f"bank{t}") for t in range(PACK)]
+        d_bank = [psum.tile([P, S], F32, name=f"d_bank{t}", tag=f"bank{PACK + t}") for t in range(PACK)]
+        for t in range(PACK):
+            product(y_bank[t][:], w_dealt[0], s_dealt[0], t, offs_words[:], offs_plane[:])
+        for t in range(PACK):
+            product(d_bank[t][:], w_dealt[1], s_dealt[1], t, hz_words[:], hz_plane[:])
+        for t in range(PACK):
+            nc.vector.tensor_scalar_mul(ys[:, t, :], y_bank[t][:], gain[:, t : t + 1])
+        for t in range(PACK):
+            nc.vector.tensor_copy(ds[:, t, :], d_bank[t][:])
+        w_dealt.append(sb("w3_dealt", [P, H], U32, tag="hz_words"))
+        nc.vector.tensor_copy(dealt_view(w_dealt[2][:].bitcast(I32)), raw_view(w_raw[2][:].bitcast(I32)))
+
+        def fetch_old(t):
+            nc.scalar.activation(old[:, t, :], page[t][:].indirect(n3_t[:]), ACT.Copy)
+
+        def entries(lst, c):
+            return lst[:, c * HALF // STRIPE : (c + 1) * HALF // STRIPE]
+
+        yg, dg = {}, {}
+
+        def fetch_results(c):
+            yg[c] = sb("yg", [P, PACK, HALF], F32)
+            dg[c] = sb("dg", [P, PACK, HALF], F32)
+            for t in range(PACK):
+                nc.scalar.activation(yg[c][:, t, :], ys[:, t, :].indirect(entries(n1_t, c)), ACT.Copy)
+            for t in range(PACK):
+                nc.scalar.activation(dg[c][:, t, :], ds[:, t, :].indirect(entries(n2_t, c)), ACT.Copy)
+
+        h_bank = {}
+
+        def third_product(c):
+            cols = slice(c * HALF, (c + 1) * HALF)
+            m1 = sb(f"m1_{c}", [P, PACK, HALF], F32, tag="step" if c else None)
+            m2 = sb(f"m2_{c}", [P, PACK, HALF], F32)
+            z = sb(f"z{c}", [P, HALF, PACK], BF16)
+            z_words = sb(f"z_words{c}", [P, HALF], U32)
+            z_plane = sb(f"z_plane{c}", [P, HALF], U8)
+            nc.vector.tensor_tensor(m2[:], yg[c][:], ds[:, :, cols], ALU.mult)
+            nc.vector.tensor_tensor(m1[:], ys[:, :, cols], dg[c][:], ALU.mult)
+            nc.vector.tensor_tensor(
+                z[:].rearrange("p (c i) t -> p c t i", i=4),
+                m1[:].rearrange("p t (c i) -> p c t i", i=4),
+                m2[:].rearrange("p t (c i) -> p c t i", i=4),
+                ALU.subtract,
+            )
+            nc.vector.quantize_mx(out=z_words[:].bitcast(FP8X4), scales=z_plane[:], in_=z[:].rearrange("p c t -> p (c t)"))
+            for u in range(2):
+                h_bank[c, u] = psum.tile([P, 2, HALF], F32, name=f"h_bank{c}{u}", tag=f"bank{2 * c + u}")
+                for e in range(2):
+                    product(h_bank[c, u][:, e, :], w_dealt[2], s_dealt[2], 2 * u + e, z_words[:], z_plane[:])
+
+        gate, nw = {}, {}
+
+        def sigmoid(c, u):
+            gate[c, u] = sb(f"gate{c}{u}", [P, 2, HALF], F32)
+            nc.scalar.activation(gate[c, u][:], h_bank[c, u][:], ACT.Tanh, scale=0.5)
+
+        def new_values(c, u):
+            was = old[:, 2 * u : 2 * u + 2, c * HALF : (c + 1) * HALF]
+            diff = sb("diff", [P, 2, HALF], F32)
+            step = sb("step", [P, 2, HALF], F32)
+            nw[c, u] = sb(f"nw{c}{u}", [P, 2, HALF], F32)
+            nc.vector.tensor_tensor(diff[:], h_bank[c, u][:], was, ALU.subtract)
+            nc.vector.scalar_tensor_tensor(step[:], gate[c, u][:], 1.0, diff[:], ALU.add, ALU.mult)
+            nc.vector.scalar_tensor_tensor(nw[c, u][:], step[:], 0.5, was, ALU.mult, ALU.add)
+
+        def put(c, t):
+            nc.scalar.activation(page[t][:].indirect(entries(n3_t, c)), nw[c, t // 2][:, t % 2, :], ACT.Copy)
+
+        woven = [sb(f"woven{v}", [P, U // 2, PACK], BF16) for v in range(2)]
+
+        def page_done(t):
+            nc.sync.dma_start(out=out_rows[:, t, :], in_=page[t][:])
+            for v in range(2):
+                nc.vector.tensor_copy(woven[v][:, :, t], page[t][:, v * U // 2 : (v + 1) * U // 2])
+
+        for t in range(PACK):
+            fetch_old(t)
+        fetch_results(0)
+        third_product(0)
+        fetch_results(1)
+        sigmoid(0, 0)
+        new_values(0, 0)
+        sigmoid(0, 1)
+        put(0, 0)
+        put(0, 1)
+        third_product(1)
+        new_values(0, 1)
+        sigmoid(1, 0)
+        sigmoid(1, 1)
+        new_values(1, 0)
+        new_values(1, 1)
+        put(0, 2)
+        put(0, 3)
+        for t in range(PACK):
+            put(1, t)
+            page_done(t)
+        out_words = sb("out_words", [P, U], U32)
+        out_plane = sb("out_plane", [P, U], U8)
+        for v in range(2):
+            cols = slice(v * U // 2, (v + 1) * U // 2)
+            nc.vector.quantize_mx(
+                out=out_words[:, cols].bitcast(FP8X4), scales=out_plane[:, cols], in_=woven[v][:].rearrange("p c t -> p (c t)")
+            )
+            nc.sync.dma_start(out=words_of(out_1)[:, cols], in_=out_words[:, cols].bitcast(I32))
+        for q in range(4):
+            queue = nc.scalar if q % 2 else nc.sync
+            queue.dma_start(out=out_2[0][4 * q : 4 * q + 4, :].bitcast(I32), in_=out_plane[32 * q : 32 * q + 4, :].bitcast(I32))

@@ -46,49 +46,45 @@ def tile_picked_twhcrossbpaget_none_po_kernel(
         xs = sb("xs", [P, T], U8)
         w_raw = [sb(f"w_raw{i}", [P, H], U32) for i in range(2)]
         w_dealt = [sb(f"w_dealt{i}", [P, H], U32) for i in range(2)]
-        s_raw = [sb(f"s_raw{i}", [P, H], U8) for i in range(2)]
+        s_raw = [sb(f"s_raw{i}", [P, H], U8) for i in range(3)]
         s_dealt = []
         gn_t = sb("gn_t", [P, PACK], F32)
         gain = sb("gain", [P, PACK], F32)
-        page = [sb(f"page{t}", [P, U], F32) for t in range(PACK)]
+        page = [sb(f"page{t}", [P, U], F32) for t in range(PACK - 1)]
         mem_rows = mem.rearrange("(p t) u -> p t u", t=PACK)
         out_rows = out_0.rearrange("(p t) u -> p t u", t=PACK)
 
         nc.vector.memset(xs[:].bitcast(I32), 0)
         nc.gpsimd.memset(s_raw[0][:].bitcast(I32), 0)
-        nc.vector.memset(s_raw[1][:].bitcast(I32), 0)
+        nc.gpsimd.memset(s_raw[1][:].bitcast(I32), 0)
+        nc.gpsimd.memset(s_raw[2][:].bitcast(I32), 0)
+
+        def load_scale_row(queue, tile, scales, a):
+            queue.dma_start(out=tile[a:P:32, :].bitcast(I32), in_=scales[0][a:16:4, :].bitcast(I32))
 
         def load_scale_rows(queue, tile, scales):
             for a in range(4):
-                queue.dma_start(out=tile[a:P:32, :].bitcast(I32), in_=scales[0][a:16:4, :].bitcast(I32))
+                load_scale_row(queue, tile, scales, a)
 
         xsc = x_scales[0]
-        nc.scalar.dma_start(out=xs[0:P:16, :].bitcast(I32), in_=xsc[0:16:2, :].bitcast(I32))
-        nc.scalar.dma_start(out=xs[1:P:16, :].bitcast(I32), in_=xsc[1:16:2, :].bitcast(I32))
-        nc.scalar.dma_start(out=xs[2:P:32, :].bitcast(I32), in_=xsc[2:16:4, :].bitcast(I32))
-        nc.scalar.dma_start(out=xs[3:P:32, :].bitcast(I32), in_=xsc[3:16:4, :].bitcast(I32))
-        load_scale_rows(nc.gpsimd, s_raw[0], w1_scales)
-        nc.sync.dma_start(hz_t[:], hz)
         nc.sync.dma_start(offs_t[:], offs)
+        nc.sync.dma_start(hz_t[:], hz)
         nc.sync.dma_start(out=gn_t[:], in_=gn.rearrange("(p t) o -> p (t o)", t=PACK))
         nc.sync.dma_start(n3_t[:], n3)
-        nc.sync.dma_start(out=xw[:].bitcast(I32), in_=words_of(x_words))
-        nc.sync.dma_start(out=w_raw[0][:].bitcast(I32), in_=words_of(w1_words))
-        nc.scalar.activation(gain[:], gn_t[:], ACT.Copy, scale=0.75)
-        nc.sync.dma_start(out=page[0][:], in_=mem_rows[:, 0, :])
         nc.sync.dma_start(n1_t[:], n1)
         nc.sync.dma_start(n2_t[:], n2)
+        nc.sync.dma_start(out=xw[:].bitcast(I32), in_=words_of(x_words))
+        nc.sync.dma_start(out=w_raw[0][:].bitcast(I32), in_=words_of(w1_words))
+        nc.sync.dma_start(out=xs[0:P:16, :].bitcast(I32), in_=xsc[0:16:2, :].bitcast(I32))
+        nc.sync.dma_start(out=xs[1:P:16, :].bitcast(I32), in_=xsc[1:16:2, :].bitcast(I32))
+        nc.sync.dma_start(out=xs[2:P:32, :].bitcast(I32), in_=xsc[2:16:4, :].bitcast(I32))
+        nc.sync.dma_start(out=xs[3:P:32, :].bitcast(I32), in_=xsc[3:16:4, :].bitcast(I32))
+        nc.scalar.activation(gain[:], gn_t[:], ACT.Copy, scale=0.75)
+        nc.sync.dma_start(out=page[0][:], in_=mem_rows[:, 0, :])
         nc.sync.dma_start(out=page[1][:], in_=mem_rows[:, 1, :])
+        load_scale_rows(nc.sync, s_raw[0], w1_scales)
         nc.sync.dma_start(out=w_raw[1][:].bitcast(I32), in_=words_of(w2_words))
-        load_scale_rows(nc.sync, s_raw[1], w2_scales)
         nc.sync.dma_start(out=page[2][:], in_=mem_rows[:, 2, :])
-        nc.sync.dma_start(out=page[3][:], in_=mem_rows[:, 3, :])
-
-        hz_bytes = sb("hz_bytes", [P, S], U8)
-        hz_plane = sb("hz_plane", [P, S], U8)
-        offs_plane = sb("offs_plane", [P, S], U8)
-        offs_words = sb("offs_words", [P, S], U32)
-        hz_words = sb("hz_words", [P, S], U32)
 
         def dealt_view(tile):
             return tile.rearrange("p (t m) -> p m t", t=PACK)
@@ -96,26 +92,28 @@ def tile_picked_twhcrossbpaget_none_po_kernel(
         def raw_view(tile):
             return tile.rearrange("p (m t) -> p m t", t=PACK)
 
+        offs_plane = sb("offs_plane", [P, S], U8)
+        offs_words = sb("offs_words", [P, S], U32)
+        hz_bytes = sb("hz_bytes", [P, S], U8)
+        hz_plane = sb("hz_plane", [P, S], U8)
         nc.vector.tensor_copy(hz_bytes[:], xs[:].indirect(hz_t[:]))
         nc.vector.tensor_copy(hz_plane[:].bitcast(I32), hz_bytes[:].bitcast(I32))
         for e in range(2):
             nc.sync.dma_start(out=hz_plane[2 + e : P : 32, :].bitcast(I32), in_=hz_bytes[16 + e : P : 32, :].bitcast(I32))
+        load_scale_rows(nc.sync, s_raw[1], w2_scales)
         nc.vector.tensor_copy(offs_plane[:], xs[:].indirect(offs_t[:]))
         nc.vector.tensor_copy(offs_words[:], xw[:].indirect(offs_t[:]))
-        s_dealt.append(sb("s1_dealt", [P, H], U8, tag="xs"))
+        s_dealt.append(sb("s1_dealt", [P, H], U8))
         nc.vector.tensor_copy(dealt_view(s_dealt[0][:]), raw_view(s_raw[0][:]))
+        hz_words = sb("hz_words", [P, S], U32, tag="s_raw0")
         nc.vector.tensor_copy(hz_words[:], xw[:].indirect(hz_t[:]))
         s_dealt.append(sb("s2_dealt", [P, H], U8, tag="hz_bytes"))
         nc.vector.tensor_copy(dealt_view(s_dealt[1][:]), raw_view(s_raw[1][:]))
         nc.scalar.copy(dealt_view(w_dealt[0][:]), raw_view(w_raw[0][:]))
         w_raw.append(sb("w_raw2", [P, H], U32, tag="w_raw0"))
-        s_raw.append(sb("s_raw2", [P, H], U8, tag="s_raw0"))
-        s_dealt.append(sb("s3_dealt", [P, H], U8))
         nc.sync.dma_start(out=w_raw[2][:].bitcast(I32), in_=words_of(w3_words))
-        nc.gpsimd.memset(s_raw[2][:].bitcast(I32), 0)
         load_scale_rows(nc.sync, s_raw[2], w3_scales)
         nc.gpsimd.tensor_copy(w_dealt[1][:].rearrange("p (t m) -> p t m", t=PACK), w_raw[1][:].rearrange("p (m t) -> p t m", t=PACK))
-        nc.gpsimd.tensor_copy(dealt_view(s_dealt[2][:]), raw_view(s_raw[2][:]))
 
         def product(out, w, w_scale, t, rhs, rhs_scale):
             cols = slice(t * P, (t + 1) * P)
@@ -126,19 +124,24 @@ def tile_picked_twhcrossbpaget_none_po_kernel(
 
         ys = sb("ys", [P, PACK, S], F32)
         ds = sb("ds", [P, PACK, S], F32)
-        old = sb("old", [P, PACK, S], F32)
         y_bank = [psum.tile([P, S], F32, name=f"y_bank{t}", tag=f"bank{t}") for t in range(PACK)]
         d_bank = [psum.tile([P, S], F32, name=f"d_bank{t}", tag=f"bank{PACK + t}") for t in range(PACK)]
         for t in range(PACK):
             product(y_bank[t][:], w_dealt[0], s_dealt[0], t, offs_words[:], offs_plane[:])
         for t in range(PACK):
+            nc.vector.tensor_scalar_mul(ys[:, t, :], y_bank[t][:], gain[:, t : t + 1])
+        s_dealt.append(sb("s3_dealt", [P, H], U8))
+        nc.gpsimd.tensor_copy(dealt_view(s_dealt[2][:]), raw_view(s_raw[2][:]))
+        for t in range(PACK):
             product(d_bank[t][:], w_dealt[1], s_dealt[1], t, hz_words[:], hz_plane[:])
         for t in range(PACK):
-            nc.vector.tensor_scalar_mul(ys[:, t, :], y_bank[t][:], gain[:, t : t + 1])
-        for t in range(PACK):
             nc.vector.tensor_copy(ds[:, t, :], d_bank[t][:])
-        w_dealt.append(sb("w3_dealt", [P, H], U32, tag="hz_words"))
+        w_dealt.append(sb("w3_dealt", [P, H], U32, tag="s_raw0"))
         nc.vector.tensor_copy(dealt_view(w_dealt[2][:].bitcast(I32)), raw_view(w_raw[2][:].bitcast(I32)))
+
+        page.append(sb("page3", [P, U], F32, tag="w_raw0"))
+        nc.sync.dma_start(out=page[3][:], in_=mem_rows[:, 3, :])
+        old = sb("old", [P, PACK, S], F32)
 
         def fetch_old(t):
             nc.scalar.activation(old[:, t, :], page[t][:].indirect(n3_t[:]), ACT.Copy)
@@ -160,9 +163,9 @@ def tile_picked_twhcrossbpaget_none_po_kernel(
 
         def third_product(c):
             cols = slice(c * HALF, (c + 1) * HALF)
-            m1 = sb(f"m1_{c}", [P, PACK, HALF], F32, tag="step" if c else None)
-            m2 = sb(f"m2_{c}", [P, PACK, HALF], F32)
-            z = sb(f"z{c}", [P, HALF, PACK], BF16)
+            m1 = sb(f"m1_{c}", [P, PACK, HALF], F32)
+            m2 = sb(f"m2_{c}", [P, PACK, HALF], F32, tag="z0" if c else None)
+            z = sb(f"z{c}", [P, HALF, PACK], BF16, tag="step00" if c else None)
             z_words = sb(f"z_words{c}", [P, HALF], U32)
             z_plane = sb(f"z_plane{c}", [P, HALF], U8)
             nc.vector.tensor_tensor(m2[:], yg[c][:], ds[:, :, cols], ALU.mult)
@@ -181,45 +184,57 @@ def tile_picked_twhcrossbpaget_none_po_kernel(
 
         gate, nw = {}, {}
 
+        diff = {}
+
+        def was(c, u):
+            return old[:, 2 * u : 2 * u + 2, c * HALF : (c + 1) * HALF]
+
+        def difference(c, u):
+            diff[c, u] = sb(f"diff{c}{u}", [P, 2, HALF], F32, tag={(0, 1): "step00", (1, 0): "step01"}.get((c, u)))
+            nc.vector.tensor_tensor(diff[c, u][:], h_bank[c, u][:], was(c, u), ALU.subtract)
+
         def sigmoid(c, u):
             gate[c, u] = sb(f"gate{c}{u}", [P, 2, HALF], F32)
             nc.scalar.activation(gate[c, u][:], h_bank[c, u][:], ACT.Tanh, scale=0.5)
 
         def new_values(c, u):
-            was = old[:, 2 * u : 2 * u + 2, c * HALF : (c + 1) * HALF]
-            diff = sb("diff", [P, 2, HALF], F32)
-            step = sb("step", [P, 2, HALF], F32)
+            step = sb(f"step{c}{u}", [P, 2, HALF], F32)
             nw[c, u] = sb(f"nw{c}{u}", [P, 2, HALF], F32)
-            nc.vector.tensor_tensor(diff[:], h_bank[c, u][:], was, ALU.subtract)
-            nc.vector.scalar_tensor_tensor(step[:], gate[c, u][:], 1.0, diff[:], ALU.add, ALU.mult)
-            nc.vector.scalar_tensor_tensor(nw[c, u][:], step[:], 0.5, was, ALU.mult, ALU.add)
+            nc.vector.scalar_tensor_tensor(step[:], gate[c, u][:], 1.0, diff[c, u][:], ALU.add, ALU.mult)
+            nc.vector.scalar_tensor_tensor(nw[c, u][:], step[:], 0.5, was(c, u), ALU.mult, ALU.add)
 
         def put(c, t):
             nc.scalar.activation(page[t][:].indirect(entries(n3_t, c)), nw[c, t // 2][:, t % 2, :], ACT.Copy)
 
-        woven = [sb(f"woven{v}", [P, U // 2, PACK], BF16) for v in range(2)]
+        woven = []
 
         def page_done(t):
             nc.sync.dma_start(out=out_rows[:, t, :], in_=page[t][:])
             for v in range(2):
                 nc.vector.tensor_copy(woven[v][:, :, t], page[t][:, v * U // 2 : (v + 1) * U // 2])
 
-        for t in range(PACK):
+        for t in range(PACK - 1):
             fetch_old(t)
         fetch_results(0)
         third_product(0)
         fetch_results(1)
+        difference(0, 0)
         sigmoid(0, 0)
         new_values(0, 0)
         sigmoid(0, 1)
+        fetch_old(PACK - 1)
         put(0, 0)
         put(0, 1)
         third_product(1)
+        difference(0, 1)
         new_values(0, 1)
-        sigmoid(1, 0)
-        sigmoid(1, 1)
-        new_values(1, 0)
-        new_values(1, 1)
+        for u in range(2):
+            sigmoid(1, u)
+        for u in range(2):
+            difference(1, u)
+            new_values(1, u)
+        woven.append(sb("woven0", [P, U // 2, PACK], BF16, tag="step11"))
+        woven.append(sb("woven1", [P, U // 2, PACK], BF16, tag="old"))
         put(0, 2)
         put(0, 3)
         for t in range(PACK):

@@ -85,6 +85,7 @@ def tile_picked_twhcrossbpaget_none_po_kernel(
         load_scale_rows(nc.sync, s_raw[0], w1_scales)
         nc.sync.dma_start(out=w_raw[1][:].bitcast(I32), in_=words_of(w2_words))
         nc.sync.dma_start(out=page[2][:], in_=mem_rows[:, 2, :])
+        load_scale_rows(nc.sync, s_raw[1], w2_scales)
 
         def dealt_view(tile):
             return tile.rearrange("p (t m) -> p m t", t=PACK)
@@ -100,20 +101,19 @@ def tile_picked_twhcrossbpaget_none_po_kernel(
         nc.vector.tensor_copy(hz_plane[:].bitcast(I32), hz_bytes[:].bitcast(I32))
         for e in range(2):
             nc.sync.dma_start(out=hz_plane[2 + e : P : 32, :].bitcast(I32), in_=hz_bytes[16 + e : P : 32, :].bitcast(I32))
-        load_scale_rows(nc.sync, s_raw[1], w2_scales)
         nc.vector.tensor_copy(offs_plane[:], xs[:].indirect(offs_t[:]))
         nc.vector.tensor_copy(offs_words[:], xw[:].indirect(offs_t[:]))
         s_dealt.append(sb("s1_dealt", [P, H], U8))
         nc.vector.tensor_copy(dealt_view(s_dealt[0][:]), raw_view(s_raw[0][:]))
         hz_words = sb("hz_words", [P, S], U32, tag="s_raw0")
         nc.vector.tensor_copy(hz_words[:], xw[:].indirect(hz_t[:]))
-        s_dealt.append(sb("s2_dealt", [P, H], U8, tag="hz_bytes"))
-        nc.vector.tensor_copy(dealt_view(s_dealt[1][:]), raw_view(s_raw[1][:]))
         nc.scalar.copy(dealt_view(w_dealt[0][:]), raw_view(w_raw[0][:]))
         w_raw.append(sb("w_raw2", [P, H], U32, tag="w_raw0"))
         nc.sync.dma_start(out=w_raw[2][:].bitcast(I32), in_=words_of(w3_words))
         load_scale_rows(nc.sync, s_raw[2], w3_scales)
-        nc.gpsimd.tensor_copy(w_dealt[1][:].rearrange("p (t m) -> p t m", t=PACK), w_raw[1][:].rearrange("p (m t) -> p t m", t=PACK))
+        w_dealt.append(sb("w_dealt2", [P, H], U32))
+        for i in (1, 2):
+            nc.gpsimd.tensor_copy(w_dealt[i][:].rearrange("p (t m) -> p t m", t=PACK), w_raw[i][:].rearrange("p (m t) -> p t m", t=PACK))
 
         def product(out, w, w_scale, t, rhs, rhs_scale):
             cols = slice(t * P, (t + 1) * P)
@@ -128,19 +128,14 @@ def tile_picked_twhcrossbpaget_none_po_kernel(
         d_bank = [psum.tile([P, S], F32, name=f"d_bank{t}", tag=f"bank{PACK + t}") for t in range(PACK)]
         for t in range(PACK):
             product(y_bank[t][:], w_dealt[0], s_dealt[0], t, offs_words[:], offs_plane[:])
+        s_dealt.append(sb("s2_dealt", [P, H], U8))
+        nc.vector.tensor_copy(dealt_view(s_dealt[1][:]), raw_view(s_raw[1][:]))
         for t in range(PACK):
             nc.vector.tensor_scalar_mul(ys[:, t, :], y_bank[t][:], gain[:, t : t + 1])
-        s_dealt.append(sb("s3_dealt", [P, H], U8))
-        nc.gpsimd.tensor_copy(dealt_view(s_dealt[2][:]), raw_view(s_raw[2][:]))
         for t in range(PACK):
             product(d_bank[t][:], w_dealt[1], s_dealt[1], t, hz_words[:], hz_plane[:])
         for t in range(PACK):
             nc.vector.tensor_copy(ds[:, t, :], d_bank[t][:])
-        w_dealt.append(sb("w3_dealt", [P, H], U32, tag="s_raw0"))
-        nc.vector.tensor_copy(dealt_view(w_dealt[2][:].bitcast(I32)), raw_view(w_raw[2][:].bitcast(I32)))
-
-        page.append(sb("page3", [P, U], F32, tag="w_raw0"))
-        nc.sync.dma_start(out=page[3][:], in_=mem_rows[:, 3, :])
         old = sb("old", [P, PACK, S], F32)
 
         def fetch_old(t):
@@ -151,11 +146,13 @@ def tile_picked_twhcrossbpaget_none_po_kernel(
 
         yg, dg = {}, {}
 
-        def fetch_results(c):
+        def fetch_y(c):
             yg[c] = sb("yg", [P, PACK, HALF], F32)
-            dg[c] = sb("dg", [P, PACK, HALF], F32)
             for t in range(PACK):
                 nc.scalar.activation(yg[c][:, t, :], ys[:, t, :].indirect(entries(n1_t, c)), ACT.Copy)
+
+        def fetch_d(c):
+            dg[c] = sb("dg", [P, PACK, HALF], F32)
             for t in range(PACK):
                 nc.scalar.activation(dg[c][:, t, :], ds[:, t, :].indirect(entries(n2_t, c)), ACT.Copy)
 
@@ -163,22 +160,34 @@ def tile_picked_twhcrossbpaget_none_po_kernel(
 
         def third_product(c):
             cols = slice(c * HALF, (c + 1) * HALF)
-            m1 = sb(f"m1_{c}", [P, PACK, HALF], F32)
-            m2 = sb(f"m2_{c}", [P, PACK, HALF], F32, tag="z0" if c else None)
+            terms = sb(f"terms{c}", [P, 2, PACK, HALF], F32, tag="z0" if c else None)
+            m1, m2 = terms[:, 0], terms[:, 1]
             z = sb(f"z{c}", [P, HALF, PACK], BF16, tag="step00" if c else None)
             z_words = sb(f"z_words{c}", [P, HALF], U32)
             z_plane = sb(f"z_plane{c}", [P, HALF], U8)
-            nc.vector.tensor_tensor(m2[:], yg[c][:], ds[:, :, cols], ALU.mult)
-            nc.vector.tensor_tensor(m1[:], ys[:, :, cols], dg[c][:], ALU.mult)
+            if c == 0:
+                for t in range(PACK):
+                    nc.gpsimd.tensor_tensor(m2[:, t, :], yg[c][:, t, :], ds[:, t, cols], ALU.mult)
+            else:
+                nc.vector.tensor_tensor(m2, yg[c][:], ds[:, :, cols], ALU.mult)
+            for t in range(PACK):
+                nc.vector.scalar_tensor_tensor(
+                    m1[:, t, :], y_bank[t][:, cols], gain[:, t : t + 1], dg[c][:, t, :], ALU.mult, ALU.mult
+                )
             nc.vector.tensor_tensor(
                 z[:].rearrange("p (c i) t -> p c t i", i=4),
-                m1[:].rearrange("p t (c i) -> p c t i", i=4),
-                m2[:].rearrange("p t (c i) -> p c t i", i=4),
+                m1.rearrange("p t (c i) -> p c t i", i=4),
+                m2.rearrange("p t (c i) -> p c t i", i=4),
                 ALU.subtract,
             )
+            if c == 0:
+                s_dealt.append(sb("s3_dealt", [P, H], U8))
+                nc.vector.tensor_copy(dealt_view(s_dealt[2][:]), raw_view(s_raw[2][:]))
+                page.append(sb("page3", [P, U], F32, tag="terms0"))
+                nc.sync.dma_start(out=page[3][:], in_=mem_rows[:, 3, :])
             nc.vector.quantize_mx(out=z_words[:].bitcast(FP8X4), scales=z_plane[:], in_=z[:].rearrange("p c t -> p (c t)"))
             for u in range(2):
-                h_bank[c, u] = psum.tile([P, 2, HALF], F32, name=f"h_bank{c}{u}", tag=f"bank{2 * c + u}")
+                h_bank[c, u] = psum.tile([P, 2, HALF], F32, name=f"h_bank{c}{u}", tag=f"bank{PACK + 2 * c + u}")
                 for e in range(2):
                     product(h_bank[c, u][:, e, :], w_dealt[2], s_dealt[2], 2 * u + e, z_words[:], z_plane[:])
 
@@ -215,11 +224,13 @@ def tile_picked_twhcrossbpaget_none_po_kernel(
 
         for t in range(PACK - 1):
             fetch_old(t)
-        fetch_results(0)
+        fetch_y(0)
+        fetch_d(0)
         third_product(0)
-        fetch_results(1)
-        difference(0, 0)
+        fetch_y(1)
+        fetch_d(1)
         sigmoid(0, 0)
+        difference(0, 0)
         new_values(0, 0)
         sigmoid(0, 1)
         fetch_old(PACK - 1)

@@ -50,7 +50,7 @@ def tile_picked_twhcrossbpaget_none_po_kernel(
         s_dealt = []
         gn_t = sb("gn_t", [P, PACK], F32)
         gain = sb("gain", [P, PACK], F32)
-        page = [sb(f"page{t}", [P, U], F32) for t in range(PACK - 1)]
+        page = [sb(f"page{t}", [P, U], F32) for t in range(PACK)]
         mem_rows = mem.rearrange("(p t) u -> p t u", t=PACK)
         out_rows = out_0.rearrange("(p t) u -> p t u", t=PACK)
 
@@ -111,6 +111,7 @@ def tile_picked_twhcrossbpaget_none_po_kernel(
         w_raw.append(sb("w_raw2", [P, H], U32, tag="w_raw0"))
         nc.sync.dma_start(out=w_raw[2][:].bitcast(I32), in_=words_of(w3_words))
         load_scale_rows(nc.sync, s_raw[2], w3_scales)
+        nc.sync.dma_start(out=page[3][:], in_=mem_rows[:, 3, :])
         w_dealt.append(sb("w_dealt2", [P, H], U32))
         for i in (1, 2):
             nc.gpsimd.tensor_copy(w_dealt[i][:].rearrange("p (t m) -> p t m", t=PACK), w_raw[i][:].rearrange("p (m t) -> p t m", t=PACK))
@@ -136,10 +137,11 @@ def tile_picked_twhcrossbpaget_none_po_kernel(
             product(d_bank[t][:], w_dealt[1], s_dealt[1], t, hz_words[:], hz_plane[:])
         for t in range(PACK):
             nc.vector.tensor_copy(ds[:, t, :], d_bank[t][:])
-        old = sb("old", [P, PACK, S], F32)
+        old = {}
 
         def fetch_old(t):
-            nc.scalar.activation(old[:, t, :], page[t][:].indirect(n3_t[:]), ACT.Copy)
+            old[t] = sb(f"old{t}", [P, S], F32, tag="z_words0" if t == PACK - 1 else None)
+            nc.scalar.activation(old[t][:], page[t][:].indirect(n3_t[:]), ACT.Copy)
 
         def entries(lst, c):
             return lst[:, c * HALF // STRIPE : (c + 1) * HALF // STRIPE]
@@ -181,10 +183,8 @@ def tile_picked_twhcrossbpaget_none_po_kernel(
                 ALU.subtract,
             )
             if c == 0:
-                s_dealt.append(sb("s3_dealt", [P, H], U8))
+                s_dealt.append(sb("s3_dealt", [P, H], U8, tag="hz_plane"))
                 nc.vector.tensor_copy(dealt_view(s_dealt[2][:]), raw_view(s_raw[2][:]))
-                page.append(sb("page3", [P, U], F32, tag="terms0"))
-                nc.sync.dma_start(out=page[3][:], in_=mem_rows[:, 3, :])
             nc.vector.quantize_mx(out=z_words[:].bitcast(FP8X4), scales=z_plane[:], in_=z[:].rearrange("p c t -> p (c t)"))
             for u in range(2):
                 h_bank[c, u] = psum.tile([P, 2, HALF], F32, name=f"h_bank{c}{u}", tag=f"bank{PACK + 2 * c + u}")
@@ -195,12 +195,13 @@ def tile_picked_twhcrossbpaget_none_po_kernel(
 
         diff = {}
 
-        def was(c, u):
-            return old[:, 2 * u : 2 * u + 2, c * HALF : (c + 1) * HALF]
+        def was(c, t):
+            return old[t][:, c * HALF : (c + 1) * HALF]
 
         def difference(c, u):
             diff[c, u] = sb(f"diff{c}{u}", [P, 2, HALF], F32, tag={(0, 1): "step00", (1, 0): "step01"}.get((c, u)))
-            nc.vector.tensor_tensor(diff[c, u][:], h_bank[c, u][:], was(c, u), ALU.subtract)
+            for e in range(2):
+                nc.vector.tensor_tensor(diff[c, u][:, e, :], h_bank[c, u][:, e, :], was(c, 2 * u + e), ALU.subtract)
 
         def sigmoid(c, u):
             gate[c, u] = sb(f"gate{c}{u}", [P, 2, HALF], F32)
@@ -208,9 +209,10 @@ def tile_picked_twhcrossbpaget_none_po_kernel(
 
         def new_values(c, u):
             step = sb(f"step{c}{u}", [P, 2, HALF], F32)
-            nw[c, u] = sb(f"nw{c}{u}", [P, 2, HALF], F32)
+            nw[c, u] = sb(f"nw{c}{u}", [P, 2, HALF], F32, tag="z_words1" if (c, u) == (0, 1) else None)
             nc.vector.scalar_tensor_tensor(step[:], gate[c, u][:], 1.0, diff[c, u][:], ALU.add, ALU.mult)
-            nc.vector.scalar_tensor_tensor(nw[c, u][:], step[:], 0.5, was(c, u), ALU.mult, ALU.add)
+            for e in range(2):
+                nc.vector.scalar_tensor_tensor(nw[c, u][:, e, :], step[:, e, :], 0.5, was(c, 2 * u + e), ALU.mult, ALU.add)
 
         def put(c, t):
             nc.scalar.activation(page[t][:].indirect(entries(n3_t, c)), nw[c, t // 2][:, t % 2, :], ACT.Copy)
@@ -245,7 +247,7 @@ def tile_picked_twhcrossbpaget_none_po_kernel(
             difference(1, u)
             new_values(1, u)
         woven.append(sb("woven0", [P, U // 2, PACK], BF16, tag="step11"))
-        woven.append(sb("woven1", [P, U // 2, PACK], BF16, tag="old"))
+        woven.append(sb("woven1", [P, U // 2, PACK], BF16, tag="z_words0"))
         put(0, 2)
         put(0, 3)
         for t in range(PACK):

from contextlib import ExitStack

import concourse.mybir as mybir

K, T, S, N, H, U = 512, 2048, 512, 512, 512, 1024
FLOPS = 3 * 2 * 512 * 512 * 512

F32 = mybir.dt.float32
BF16 = mybir.dt.bfloat16
I32 = mybir.dt.int32
U32 = mybir.dt.uint32
U16 = mybir.dt.uint16
U8 = mybir.dt.uint8
FP8X4 = mybir.dt.float8_e4m3fn_x4
ACT = mybir.ActivationFunctionType
ALU = mybir.AluOpType

P = 128
PACK = 4
HALF = S // 2
STRIPE = 16


def tile_picked_twhcrossbpaget_none_po_kernel(
    tc, x_words, x_scales, w1_words, w1_scales, w2_words, w2_scales, gn, w3_words, w3_scales, mem, offs, hz, n1, n2, n3,
    out_0, out_1, out_2,
):
    nc = tc.nc

    def words_of(packed):
        return packed[0].rearrange("p n r -> p (n r)").bitcast(I32)

    with ExitStack() as ctx:
        keep = ctx.enter_context(tc.tile_pool(name="keep", bufs=1))
        psum = ctx.enter_context(tc.psum_pool(name="psum", bufs=1))

        def sb(name, shape, dtype, tag=None):
            return keep.tile(shape, dtype, name=name, tag=tag or name, align_bytes=64)

        offs_t = sb("offs_t", [P, S // STRIPE], U16)
        hz_t = sb("hz_t", [P, S // STRIPE], U16)
        n1_t = sb("n1_t", [P, S // STRIPE], U16)
        n2_t = sb("n2_t", [P, S // STRIPE], U16)
        n3_t = sb("n3_t", [P, S // STRIPE], U16)
        xw = sb("xw", [P, T], U32)
        xs = sb("xs", [P, T], U8)
        w_raw = [sb(f"w_raw{i}", [P, H], U32) for i in range(2)]
        w_dealt = [sb(f"w_dealt{i}", [P, H], U32) for i in range(2)]
        s_raw = [sb(f"s_raw{i}", [P, H], U8) for i in range(3)]
        s_dealt = []
        gn_t = sb("gn_t", [P, PACK], F32)
        gain = sb("gain", [P, PACK], F32)
        page = [sb(f"page{t}", [P, U], F32) for t in range(PACK)]
        mem_rows = mem.rearrange("(p t) u -> p t u", t=PACK)
        out_rows = out_0.rearrange("(p t) u -> p t u", t=PACK)

        nc.vector.memset(xs[:].bitcast(I32), 0)
        nc.gpsimd.memset(s_raw[0][:].bitcast(I32), 0)
        nc.gpsimd.memset(s_raw[1][:].bitcast(I32), 0)
        nc.gpsimd.memset(s_raw[2][:].bitcast(I32), 0)

        def load_scale_row(queue, tile, scales, a):
            queue.dma_start(out=tile[a:P:32, :].bitcast(I32), in_=scales[0][a:16:4, :].bitcast(I32))

        def load_scale_rows(queue, tile, scales):
            for a in range(4):
                load_scale_row(queue, tile, scales, a)

        xsc = x_scales[0]
        nc.sync.dma_start(offs_t[:], offs)
        nc.sync.dma_start(hz_t[:], hz)
        nc.sync.dma_start(out=gn_t[:], in_=gn.rearrange("(p t) o -> p (t o)", t=PACK))
        nc.sync.dma_start(n3_t[:], n3)
        nc.sync.dma_start(n1_t[:], n1)
        nc.sync.dma_start(n2_t[:], n2)
        nc.sync.dma_start(out=xw[:].bitcast(I32), in_=words_of(x_words))
        nc.sync.dma_start(out=w_raw[0][:].bitcast(I32), in_=words_of(w1_words))
        nc.sync.dma_start(out=xs[0:P:16, :].bitcast(I32), in_=xsc[0:16:2, :].bitcast(I32))
        nc.sync.dma_start(out=xs[1:P:16, :].bitcast(I32), in_=xsc[1:16:2, :].bitcast(I32))
        nc.sync.dma_start(out=xs[2:P:32, :].bitcast(I32), in_=xsc[2:16:4, :].bitcast(I32))
        nc.sync.dma_start(out=xs[3:P:32, :].bitcast(I32), in_=xsc[3:16:4, :].bitcast(I32))
        nc.scalar.activation(gain[:], gn_t[:], ACT.Copy, scale=0.75)
        nc.sync.dma_start(out=page[0][:], in_=mem_rows[:, 0, :])
        nc.sync.dma_start(out=page[1][:], in_=mem_rows[:, 1, :])
        load_scale_rows(nc.sync, s_raw[0], w1_scales)
        nc.sync.dma_start(out=w_raw[1][:].bitcast(I32), in_=words_of(w2_words))
        nc.sync.dma_start(out=page[2][:], in_=mem_rows[:, 2, :])
        load_scale_rows(nc.sync, s_raw[1], w2_scales)

        def dealt_view(tile):
            return tile.rearrange("p (t m) -> p m t", t=PACK)

        def raw_view(tile):
            return tile.rearrange("p (m t) -> p m t", t=PACK)

        offs_plane = sb("offs_plane", [P, S], U8)
        offs_words = sb("offs_words", [P, S], U32)
        hz_bytes = sb("hz_bytes", [P, S], U8)
        hz_plane = sb("hz_plane", [P, S], U8)
        nc.vector.tensor_copy(hz_bytes[:], xs[:].indirect(hz_t[:]))
        nc.vector.tensor_copy(hz_plane[:].bitcast(I32), hz_bytes[:].bitcast(I32))
        for e in range(2):
            nc.sync.dma_start(out=hz_plane[2 + e : P : 32, :].bitcast(I32), in_=hz_bytes[16 + e : P : 32, :].bitcast(I32))
        nc.vector.tensor_copy(offs_plane[:], xs[:].indirect(offs_t[:]))
        nc.vector.tensor_copy(offs_words[:], xw[:].indirect(offs_t[:]))
        s_dealt.append(sb("s1_dealt", [P, H], U8))
        nc.vector.tensor_copy(dealt_view(s_dealt[0][:]), raw_view(s_raw[0][:]))
        hz_words = sb("hz_words", [P, S], U32, tag="s_raw0")
        nc.vector.tensor_copy(hz_words[:], xw[:].indirect(hz_t[:]))
        nc.scalar.copy(dealt_view(w_dealt[0][:]), raw_view(w_raw[0][:]))
        w_raw.append(sb("w_raw2", [P, H], U32, tag="w_raw0"))
        nc.sync.dma_start(out=w_raw[2][:].bitcast(I32), in_=words_of(w3_words))
        load_scale_rows(nc.sync, s_raw[2], w3_scales)
        nc.sync.dma_start(out=page[3][:], in_=mem_rows[:, 3, :])
        w_dealt.append(sb("w_dealt2", [P, H], U32))
        for i in (1, 2):
            nc.gpsimd.tensor_copy(w_dealt[i][:].rearrange("p (t m) -> p t m", t=PACK), w_raw[i][:].rearrange("p (m t) -> p t m", t=PACK))

        def product(out, w, w_scale, t, rhs, rhs_scale):
            cols = slice(t * P, (t + 1) * P)
            nc.tensor.matmul_mx(
                out=out, lhsT=w[:, cols].bitcast(FP8X4), lhsT_scale=w_scale[:, cols],
                rhs=rhs.bitcast(FP8X4), rhs_scale=rhs_scale, start=True, stop=True,
            )

        ys = sb("ys", [P, PACK, S], F32)
        ds = sb("ds", [P, PACK, S], F32)
        y_bank = [psum.tile([P, S], F32, name=f"y_bank{t}", tag=f"bank{t}") for t in range(PACK)]
        d_bank = [psum.tile([P, S], F32, name=f"d_bank{t}", tag=f"bank{PACK + t}") for t in range(PACK)]
        for t in range(PACK):
            product(y_bank[t][:], w_dealt[0], s_dealt[0], t, offs_words[:], offs_plane[:])
        s_dealt.append(sb("s2_dealt", [P, H], U8))
        nc.vector.tensor_copy(dealt_view(s_dealt[1][:]), raw_view(s_raw[1][:]))
        for t in range(PACK):
            nc.vector.tensor_scalar_mul(ys[:, t, :], y_bank[t][:], gain[:, t : t + 1])
        for t in range(PACK):
            product(d_bank[t][:], w_dealt[1], s_dealt[1], t, hz_words[:], hz_plane[:])
        for t in range(PACK):
            nc.vector.tensor_copy(ds[:, t, :], d_bank[t][:])
        old = {}

        def fetch_old(t):
            old[t] = sb(f"old{t}", [P, S], F32, tag="z_words0" if t == PACK - 1 else None)
            nc.scalar.activation(old[t][:], page[t][:].indirect(n3_t[:]), ACT.Copy)

        def entries(lst, c):
            return lst[:, c * HALF // STRIPE : (c + 1) * HALF // STRIPE]

        yg, dg = {}, {}

        def fetch_y(c):
            yg[c] = sb("yg", [P, PACK, HALF], F32)
            for t in range(PACK):
                nc.scalar.activation(yg[c][:, t, :], ys[:, t, :].indirect(entries(n1_t, c)), ACT.Copy)

        def fetch_d(c):
            dg[c] = sb("dg", [P, PACK, HALF], F32)
            for t in range(PACK):
                nc.scalar.activation(dg[c][:, t, :], ds[:, t, :].indirect(entries(n2_t, c)), ACT.Copy)

        h_bank = {}

        def third_product(c):
            cols = slice(c * HALF, (c + 1) * HALF)
            terms = sb(f"terms{c}", [P, 2, PACK, HALF], F32, tag="z0" if c else None)
            m1, m2 = terms[:, 0], terms[:, 1]
            z = sb(f"z{c}", [P, HALF, PACK], BF16, tag="step00" if c else None)
            z_words = sb(f"z_words{c}", [P, HALF], U32)
            z_plane = sb(f"z_plane{c}", [P, HALF], U8)
            if c == 0:
                for t in range(PACK):
                    nc.gpsimd.tensor_tensor(m2[:, t, :], yg[c][:, t, :], ds[:, t, cols], ALU.mult)
            else:
                nc.vector.tensor_tensor(m2, yg[c][:], ds[:, :, cols], ALU.mult)
            for t in range(PACK):
                nc.vector.scalar_tensor_tensor(
                    m1[:, t, :], y_bank[t][:, cols], gain[:, t : t + 1], dg[c][:, t, :], ALU.mult, ALU.mult
                )
            nc.vector.tensor_tensor(
                z[:].rearrange("p (c i) t -> p c t i", i=4),
                m1.rearrange("p t (c i) -> p c t i", i=4),
                m2.rearrange("p t (c i) -> p c t i", i=4),
                ALU.subtract,
            )
            if c == 0:
                s_dealt.append(sb("s3_dealt", [P, H], U8, tag="hz_plane"))
                nc.vector.tensor_copy(dealt_view(s_dealt[2][:]), raw_view(s_raw[2][:]))
            nc.vector.quantize_mx(out=z_words[:].bitcast(FP8X4), scales=z_plane[:], in_=z[:].rearrange("p c t -> p (c t)"))
            for u in range(2):
                h_bank[c, u] = psum.tile([P, 2, HALF], F32, name=f"h_bank{c}{u}", tag=f"bank{PACK + 2 * c + u}")
                for e in range(2):
                    product(h_bank[c, u][:, e, :], w_dealt[2], s_dealt[2], 2 * u + e, z_words[:], z_plane[:])

        gate, nw = {}, {}

        diff = {}

        def was(c, t):
            return old[t][:, c * HALF : (c + 1) * HALF]

        def difference(c, u):
            diff[c, u] = sb(f"diff{c}{u}", [P, 2, HALF], F32, tag={(0, 1): "step00", (1, 0): "step01"}.get((c, u)))
            for e in range(2):
                nc.vector.tensor_tensor(diff[c, u][:, e, :], h_bank[c, u][:, e, :], was(c, 2 * u + e), ALU.subtract)

        def sigmoid(c, u):
            gate[c, u] = sb(f"gate{c}{u}", [P, 2, HALF], F32)
            nc.scalar.activation(gate[c, u][:], h_bank[c, u][:], ACT.Tanh, scale=0.5)

        def new_values(c, u):
            step = sb(f"step{c}{u}", [P, 2, HALF], F32)
            nw[c, u] = sb(f"nw{c}{u}", [P, 2, HALF], F32, tag="z_words1" if (c, u) == (0, 1) else None)
            nc.vector.scalar_tensor_tensor(step[:], gate[c, u][:], 1.0, diff[c, u][:], ALU.add, ALU.mult)
            for e in range(2):
                nc.vector.scalar_tensor_tensor(nw[c, u][:, e, :], step[:, e, :], 0.5, was(c, 2 * u + e), ALU.mult, ALU.add)

        def put(c, t):
            nc.scalar.activation(page[t][:].indirect(entries(n3_t, c)), nw[c, t // 2][:, t % 2, :], ACT.Copy)

        woven = []

        def page_done(t):
            nc.sync.dma_start(out=out_rows[:, t, :], in_=page[t][:])
            for v in range(2):
                nc.vector.tensor_copy(woven[v][:, :, t], page[t][:, v * U // 2 : (v + 1) * U // 2])

        for t in range(PACK - 1):
            fetch_old(t)
        fetch_y(0)
        fetch_d(0)
        third_product(0)
        fetch_y(1)
        fetch_d(1)
        sigmoid(0, 0)
        difference(0, 0)
        new_values(0, 0)
        sigmoid(0, 1)
        fetch_old(PACK - 1)
        put(0, 0)
        put(0, 1)
        third_product(1)
        difference(0, 1)
        new_values(0, 1)
        for u in range(2):
            sigmoid(1, u)
        for u in range(2):
            difference(1, u)
            new_values(1, u)
        woven.append(sb("woven0", [P, U // 2, PACK], BF16, tag="step11"))
        woven.append(sb("woven1", [P, U // 2, PACK], BF16, tag="z_words0"))
        put(0, 2)
        put(0, 3)
        for t in range(PACK):
            put(1, t)
            page_done(t)
        out_words = sb("out_words", [P, U], U32)
        out_plane = sb("out_plane", [P, U], U8)
        for v in range(2):
            cols = slice(v * U // 2, (v + 1) * U // 2)
            nc.vector.quantize_mx(
                out=out_words[:, cols].bitcast(FP8X4), scales=out_plane[:, cols], in_=woven[v][:].rearrange("p c t -> p (c t)")
            )
            nc.sync.dma_start(out=words_of(out_1)[:, cols], in_=out_words[:, cols].bitcast(I32))
        for q in range(4):
            queue = nc.scalar if q % 2 else nc.sync
            queue.dma_start(out=out_2[0][4 * q : 4 * q + 4, :].bitcast(I32), in_=out_plane[32 * q : 32 * q + 4, :].bitcast(I32))
